import numpy as np, ml_dtypes
CORES = [6,15,38,47]
N = 4
BF = ml_dtypes.bfloat16
W, L, CAP, T, D = 8192, 256, 2, 5, 1
def place(s, p):
    return ((((s & 4095) * (2 * p + 1)) >> 3) + 37 * s + 613 * p) & (W - 1)
def cells(lf, p):
    return place((32768 + lf)[..., None] >> np.arange(16), p[..., None])
def page(w, z):
    return np.add.reduce(w[..., 0:1] * z, axis=-2) & 255
def pack(x, c, z, lf, w, th):
    return {"x0": x.reshape(N, 128, W).astype(np.float32).astype(BF), "c0": c.reshape(N, 8, W).astype(np.float32).astype(BF), "z0": z.reshape(N, 128, L).astype(np.float32).astype(BF),
            "leaf": np.ascontiguousarray(lf).astype(np.int32), "wt": np.ascontiguousarray(w.reshape(N, 128, 2)).astype(np.int32), "th": np.ascontiguousarray(th.reshape(N, 8, 1)).astype(np.int32)}
def parts(rng):
    x = rng.integers(0, 16, (N, 8, 16, W)); c = rng.integers(0, CAP, (N, 8, W))
    pool = rng.integers(0, 16, (N, 8, 16, 64)); z = np.take_along_axis(pool, rng.integers(0, 64, (N, 8, 1, L)), 3)
    z = np.where(rng.random((N, 8, 1, L)) < 0.5, z, rng.integers(0, 16, (N, 8, 16, L)))
    few = rng.integers(0, 32768, (N, 8, 16)); lf = np.take_along_axis(few, rng.integers(0, 16, (N, 8, L)), 2)
    lf = np.where(rng.random((N, 8, L)) < 0.25, lf, rng.integers(0, 32768, (N, 8, L)))
    return x, c, z, lf, rng.integers(1, 256, (N, 8, 16, 2)), rng.integers(50, 81, (N, 8))
def setup_inputs(rng):
    return pack(*parts(rng))
def setup_inputs_spread(rng):
    def uneven(n):
        v = np.minimum((np.exp2(4 * rng.random((N, 8, 1, n))) * rng.random((N, 8, 16, n))).astype(np.int64), 15)
        return np.where(rng.random((N, 8, 1, n)) < 0.5, v, 15 - v)
    c = np.where(rng.random((N, 8, W)) < rng.random((N, 8, 1)), CAP - 1, rng.integers(0, CAP, (N, 8, W)))
    lf = np.minimum(np.exp2(15 * rng.random((N, 8, L))).astype(np.int64), 32767)
    w = np.minimum(np.maximum(np.exp2(8 * rng.random((N, 8, 16, 2))).astype(np.int64), 1), 255)
    return pack(uneven(W), c, uneven(L), lf, w, rng.integers(0, 121, (N, 8)))
def setup_inputs_ends(rng):
    def ends(n):
        one = rng.integers(0, 2, (N, 8, 1, n)); el = rng.integers(0, 2, (N, 8, 16, n))
        return np.where(rng.random((N, 8, 1, n)) < 0.5, one, el) * 15
    x = ends(W); z = ends(L); c = (CAP - 1) * rng.integers(0, 2, (N, 8, W)); lf = 32767 * rng.integers(0, 2, (N, 8, L))
    w = 1 + 254 * rng.integers(0, 2, (N, 8, 16, 2)); w[:, 1::3] = 255; w[:, 0, 0] = 1; w[:, 0, 15] = 255
    th = 120 * ((np.arange(8)[None, :] + rng.integers(0, 2, (N, 1))) & 1)
    for q in range(N):
        for g in range(8):
            if g % 3 == 1:
                z[q, g][:, [1, L - 2]] = 15; lf[q, g, [1, L - 2]] = 32767
                x[q, g][:, cells(np.array([32767]), np.array([(16 * 15 * 255) & 255]))[0]] = 0
            z[q, g][:, [2, L - 3]] = 0; lf[q, g, [2, L - 3]] = 0
            order = rng.permutation(16)
            for m in (16, 0) + tuple(range(1, 16)):
                v = 15 * (order < m).astype(np.int64); p = int(np.dot(w[q, g, :, 0], v)) & 255
                k = np.flatnonzero(place(32768 + np.arange(32768), p) == W - 1)
                if k.size:
                    lone = int(rng.choice(k))
                    z[q, g][:, [0, L - 1]] = v[:, None]; lf[q, g, [0, L - 1]] = lone
                    x[q, g][:, W - 1] = v if (q + g) % 2 == 0 else 15 - v
                    above = int(place((32768 + lone) >> 1, p))
                    if (q + g) % 2 == 1 and above != W - 1:
                        x[q, g][:, above] = v; c[q, g, W - 1] = CAP - 1
                    break
    return pack(x, c, z, lf, w, th)
def near(z, n):
    i = np.arange(16)[:, None]; d = (n >> 4)[None, :] + (i < (n & 15)[None, :])
    return np.where(z < 8, z + d, z - d)
def setup_inputs_corners(rng):
    x, c, z, lf, w, th = parts(rng)
    th = rng.choice(np.array([0, 1, 20, 40, 120]), (N, 8)); kind = (np.arange(8)[None, :] + rng.integers(0, 3, (N, 1))) % 3
    c = np.where(kind[:, :, None] == 0, 0, np.where(kind[:, :, None] == 1, CAP - 1, c))
    lf = np.where(rng.random((N, 8, L)) < 0.5, rng.choice(np.array([0, 1, 16383, 16384, 32766, 32767]), (N, 8, L)), lf); lf[:, :, 0] = 0; lf[:, :, L - 1] = 32767
    wk = rng.integers(0, 4, (N, 8, 1, 2)); w = np.where(wk == 0, 1, np.where(wk == 1, 255, w))
    zk = rng.random((N, 8, 1, L)); z = np.where(zk < 0.05, 0, np.where(zk > 0.95, 15, z))
    for q in range(N):
        for g in range(8):
            h = cells(lf[q, g], page(w[q, g], z[q, g]))
            lv = rng.choice(np.array([0, 1, 7, 14]), L); n = np.maximum(th[q, g] + rng.integers(-1, 2, L), 0)
            x[q, g][:, h[np.arange(L), lv]] = near(z[q, g], n)
            e = np.array([th[q, g], th[q, g] + 1])
            x[q, g][:, h[[0, L - 1], 0]] = near(z[q, g][:, [0, L - 1]], e)
    return pack(x, c, z, lf, w, th)
def setup_inputs_crowd(rng):
    x, c, z, lf, w, th = parts(rng)
    for q in range(N):
        if q % 3 < 2:
            x[q] = rng.integers(0, 4, (8, 16, W)); z[q] = rng.integers(12, 16, (8, 16, L)); th[q] = rng.integers(0, 61, 8)
        lone = 0 if q & 1 else L - 1
        for g in range(8):
            if g % 4 == 0: ix = np.full(L, int(rng.integers(0, L)))
            elif g % 4 == 1: ix = np.full(L, lone ^ 1); ix[lone] = lone
            elif g % 4 == 2: ix = rng.integers(0, 4, L)
            else: ix = np.arange(L)
            z[q, g] = z[q, g][:, ix]; lf[q, g] = lf[q, g][ix]
            if q % 3 == 1 and g == 1:
                pg = page(w[q, g], z[q, g]); other = cells(lf[q, g, [lone ^ 1]], pg[[lone ^ 1]])[0]
                some = rng.permutation(32768)[:256]; hs = place(32768 + some, pg[lone])
                k = int(np.argmax(~np.isin(hs, other)))
                lf[q, g, lone] = some[k]; x[q, g][:, hs[k]] = z[q, g][:, lone]
    return pack(x, c, z, lf, w, th)
def setup_inputs_full(rng):
    x, c, z, lf, w, th = parts(rng); th = rng.integers(0, 9, (N, 8)); c[:, [0, 1, 4, 5]] = CAP - 1
    for q in range(N):
        for g in range(8):
            a, b = rng.permutation(16)[:2]; w[q, g, a, 0] = 1; w[q, g, b, 0] = 16
            zz = rng.integers(0, 16, (16, L)); zz[[a, b]] = 0
            pg = np.full(L, int(rng.integers(0, 256))) if g % 4 == 3 else rng.permutation(256)[:L]
            left = (pg - page(w[q, g], zz)) & 255; zz[a] = left & 15; zz[b] = left >> 4; z[q, g] = zz
            cand = rng.integers(0, 32768, (L, 24)); lv = rng.integers(1, 16, (L, 24))
            if g % 2 == 0: lv[:, :16] = 15
            h = cells(cand, pg[:, None]).tolist(); lv = lv.tolist(); taken = set(); hits = set(); at = []; who = []
            for l in range(L):
                for m in range(24):
                    v = lv[l][m]; way = h[l][m]
                    if way[v - 1] not in taken and (v == 15 or (way[v] not in hits and way[v] not in way[:v])): break
                lf[q, g, l] = cand[l, m]; taken.add(way[v - 1])
                if v < 15: hits.add(way[v]); at.append(way[v]); who.append(l)
            if at: x[q, g][:, np.array(at)] = near(zz[:, np.array(who)], rng.integers(0, int(th[q, g]) + 1, len(at)))
    return pack(x, c, z, lf, w, th)
def check_inputs(d):
    bad = []
    for k, lo, hi in (("x0", 0, 15), ("c0", 0, CAP - 1), ("z0", 0, 15), ("leaf", 0, 32767), ("wt", 1, 255), ("th", 0, 120)):
        a = np.asarray(d[k]).astype(np.float64)
        if not (np.min(a) >= lo and np.max(a) <= hi): bad.append("range of " + k)
        elif np.any(a != np.floor(a)): bad.append("whole numbers in " + k)
    return bad
def reference(x0, c0, z0, leaf, wt, th):
    X = x0.astype(np.float32).astype(np.int64).reshape(N, 8, 16, W); C = c0.astype(np.float32).astype(np.int64).reshape(N, 8, W)
    z = z0.astype(np.float32).astype(np.int64).reshape(N, 8, 16, L); lf = leaf.astype(np.int64)
    w = wt.astype(np.int64).reshape(N, 8, 16, 2); lim = th.astype(np.int64).reshape(N, 8, 1, 1); A = np.zeros(N, np.int64); zs = []
    for t in range(T):
        home = (np.arange(N) - D * t) % N
        zq = z[home]; lq = lf[home]
        h = cells(lq, page(w, zq))
        xk = np.take_along_axis(X, h.reshape(N, 8, 1, L * 16), 3).reshape(N, 8, 16, L, 16)
        dist = np.add.reduce(np.abs(xk - zq[..., None]), axis=2)
        hit = dist <= lim + (A & 15).reshape(N, 1, 1, 1); hit[..., 15] = True
        j = np.argmax(hit, axis=-1)
        y = np.take_along_axis(xk, j[:, :, None, :, None], 4)[..., 0]
        for q in range(N):
            for g in range(8):
                m = np.flatnonzero(j[q, g] > 0); named = h[q, g, m, j[q, g, m] - 1]
                cell, first = np.unique(named, return_index=True); who = m[first]
                C[q, g, cell] += 1; full = C[q, g, cell] == CAP
                X[q, g][:, cell[full]] = y[q, g][:, who[full]]; C[q, g, cell[full]] = 0
                cell, first = np.unique(h[q, g, :, 15], return_index=True)
                X[q, g][:, cell] = (xk[q, g][:, first, 15] + zq[q, g][:, first]) >> 1
        A = np.add.reduce((j == 15).astype(np.int64).reshape(N, 8 * L), axis=1)
        zq = np.abs(zq - y); z = np.zeros_like(zq); z[home] = zq; zs.append(z)
        if t < T - 1: lf[home] = (8 * lq + np.add.reduce(w[..., 1:2] * zq, axis=2)) & 32767
    return {"zs": np.concatenate(zs, axis=3).reshape(N, 128, T * L).astype(np.float32).astype(BF), "xs": np.add.reduce(w[..., 0:1] * X, axis=2).astype(np.float32), "cs": C.astype(np.float32)}

from concourse.mybir import AluOpType, ActivationFunctionType, AxisListType

CB = 8208
NW = 16416
B2, F4, I4, U2 = "bfloat16", "float32", "int32", "uint16"
SCRATCH = {"win": ("sbuf", [128, NW], B2), "sh": ("sbuf", [128, 15, 8, 16], B2), "vals": ("sbuf", [128, 16, 32], B2),
           "diff": ("sbuf", [128, 4096], B2),
           "ad": ("sbuf", [128, 256, 16], B2),
           "eye": ("sbuf", [128, 8, 16], B2), "neye": ("sbuf", [128, 8, 16], B2), "lh": ("sbuf", [128, 8, 128], B2),
           "wd": ("sbuf", [128, 16, 128], B2),
           "xa": ("sbuf", [128, 16, 128], B2),
           "eq": ("sbuf", [128, 15, 32], B2), "ts": ("sbuf", [128, 4, 2, 4, 4], F4), "oi": ("sbuf", [128, 4, 2, 4], I4),
           "pg": ("psum", [128, 4, 8, 16], F4), "pd": ("psum", [128, 32, 16], F4), "pq": ("psum", [128, 16, 32], F4),
           "pf": ("psum", [128, 512], F4), "pn": ("psum", [128, 512], F4), "pr": ("psum", [128, 512], F4),
           "px": ("psum", [128, 512], F4)}
for _d, _l in ((B2, "ones:128 blk1:128 blk:128 eye2:128 zz:16 thb:1 j15:16 hl:64 rw:256 rv:256 zh1:256 zh2:256 z2:256 yv:256 nc:256"),
               (F4, "p15:1 gp1:1 gp0:1 wf:2 wp:2 thc:1 mc:1 lu:32 lt:32 e16:16 e3:256 hc:256 rr:256 b8:64 sp:256 aa:256 hf:256 "
                    "hd:256 ms:256 sc:256 sn:256 ac:1 nr:32 uu:32 u2:16 un:32 ur:16 xo:512"),
               (I4, "pidx:1 p15i:1 gpi:1 wti:2 thi:1 lfi:16 qi:16 fi:16 ss:256 bi:64 ww:256 hh:256 ai:1 am:1 ri:16 rn:16"),
               (U2, "li:256 lo:16 nl:16 rl:32 rt:32")):
    for _x in _l.split():
        SCRATCH[_x.split(":")[0]] = ("sbuf", [128, int(_x.split(":")[1])], _d)
for _t in range(5):
    SCRATCH["zi%d" % _t] = ("sbuf", [128, 4, 4, 16], B2)
    SCRATCH["zn%d" % _t] = ("sbuf", [128, 256], B2)
    SCRATCH["fw%d" % _t] = ("sbuf", [128, 4, 2, 4], F4)
    SCRATCH["add%d" % _t] = ("sbuf", [128, 4, 2, 4], F4)
SEMAPHORES = ["qv", "qt", "qs", "qg", "ls", "wp", "gd", "dc", "h1", "h2"] + ["za%d" % t for t in range(1, 5)] + \
    ["fa%d" % t for t in range(1, 5)] + ["d%d" % k for k in range(12)]


def state(g, T):
    return {"g": g, "T": T, "q": {"v": g.vector, "t": g.tensor, "s": g.scalar, "g": g, "y": g.sync},
            "known": {k: {} for k in "vtsgy"}, "count": {}, "w": {}, "r": {}, "nd": 0}


def norm(x):
    return (x, 0, 1 << 30) if isinstance(x, str) else x


def need(S, q, ev):
    kn = S["known"][q]
    sem, val, clock = ev
    if kn.get(sem, 0) >= val:
        return
    S["q"][q].wait_ge(S["T"].sem[sem], val)
    for k in clock:
        kn[k] = max(kn.get(k, 0), clock[k])
    kn[sem] = max(kn.get(sem, 0), val)


def deps(S, q, reads, writes):
    todo = []
    for x, old in [(x, S["w"]) for x in reads] + [(x, S["w"]) for x in writes] + [(x, S["r"]) for x in writes]:
        n, lo, hi = norm(x)
        for (a, b, ev) in old.get(n, []):
            if lo < b and a < hi and not (q == "t" and ev[0] == "qt"):
                todo.append(ev)
    for ev in sorted(todo, key=lambda e: -e[1]):
        need(S, q, ev)


def note(S, reads, writes, ev):
    for x in reads:
        n, lo, hi = norm(x)
        l = S["r"].setdefault(n, [])
        l[:] = [e for e in l if not (e[2][0] == ev[0] and lo <= e[0] and e[1] <= hi)] + [(lo, hi, ev)]
    for x in writes:
        n, lo, hi = norm(x)
        for key in ("w", "r"):
            l = S[key].setdefault(n, [])
            l[:] = [e for e in l if not (lo <= e[0] and e[1] <= hi)]
        S["w"][n].append((lo, hi, ev))


def op(S, q, fn, reads, writes):
    deps(S, q, reads, writes)
    sem = "q" + q
    S["count"][sem] = S["count"].get(sem, 0) + 1
    fn().then_inc(S["T"].sem[sem], 1)
    clock = dict(S["known"][q])
    clock[sem] = S["count"][sem]
    note(S, reads, writes, (sem, S["count"][sem], clock))


def dma(S, q, fn, reads, writes, sem=None, parts=1):
    deps(S, q, reads, writes)
    if sem is None:
        sem = "d%d" % S["nd"]
        S["nd"] += 1
    for k in range(parts):
        (fn(k) if parts > 1 else fn()).then_inc(S["T"].sem[sem], 16)
    clock = dict(S["known"][q])
    clock[sem] = S["count"][sem] = 16 * parts
    note(S, reads, writes, (sem, 16 * parts, clock))


def arrival(S, sem, val, writes):
    S["count"][sem] = val
    note(S, [], writes, (sem, val, {}))


def rank_program(g, core, T, topo):
    rank = T.rank_of(core)
    if rank is None:
        return
    A, F = AluOpType, ActivationFunctionType
    S = state(g, T)
    V, P, C = g.vector, g.tensor, g.scalar
    cores = list(T.cores)
    N = len(cores)
    nxt, prv = cores[(rank + 1) % N], cores[(rank - 1) % N]
    E = len(topo.engines(prv, core))

    def v(fn, reads, writes):
        op(S, "v", fn, reads, writes)

    def s(fn, reads, writes):
        op(S, "s", fn, reads, writes)

    def vs(o, i, a, b, p, q, reads, writes):
        if q is None:
            v(lambda: V.tensor_scalar(o, i, a, b, p), reads, writes)
        else:
            v(lambda: V.tensor_scalar(o, i, a, b, p, q), reads, writes)

    def vt(o, x, y, p, reads, writes):
        v(lambda: V.tensor_tensor(o, x, y, p), reads, writes)

    def copy(o, i, reads, writes, bias=0.0, scale=1.0):
        s(lambda: C.activation(o, i, F.Copy, bias=bias, scale=scale), reads, writes)

    def mm(out, lhsT, rhs, start, stop, reads, writes):
        op(S, "t", lambda: P.matmul(out, lhsT, rhs, start=start, stop=stop), reads, writes)

    def send(dst, out, src, sem, reads):
        deps(S, "g", reads, [])
        rid, pid, _ = topo.addr(dst)
        g.remote_dma(out, src, T.sem[sem], T.sem.ls, pid, rid, topo.mask(core, dst))
        S["count"]["ls"] = S["count"].get("ls", 0) + len(topo.engines(core, dst))

    dma(S, "y", lambda: g.sync.dma_start(T.wti[:], T.wt[:]), [], ["wti"])
    dma(S, "s", lambda: C.dma_start(T.lfi[:], T.leaf[:]), [], ["lfi"])
    dma(S, "y", lambda: g.sync.dma_start(T.zi0[:], T.z0[:]), [], ["zi0"])
    dma(S, "y", lambda: g.sync.dma_start(T.win[:, 16:CB], T.x0[:]), [], [("win", 16, CB)])
    dma(S, "y", lambda i: g.sync.dma_start(T.win[i:128:16, CB + 16:NW], T.c0[:]), [], [("win", CB + 16, NW)], "dc", 16)
    op(S, "g", lambda: g.iota(T.pidx[:], [[0, 1]], 0, 1), [], ["pidx"])
    for n, x in [("ones", 1.0), ("thi", 0), ("lh", 0.0), ("add0", 1.0), ("wd", 0.0), ("zz", 0.0), ("e3", -256.0), ("hd", 0.0)] + \
            [("fw%d" % t, 1.0) for t in range(4)]:
        v(lambda: V.memset(T[n][:], x), [], [n])
    v(lambda: V.memset(T.win[:, 0:16], 0.0), [], [("win", 0, 16)])
    v(lambda: V.memset(T.win[:, CB:CB + 16], 0.0), [], [("win", CB, CB + 16)])
    dma(S, "s", lambda: C.dma_start(T.thi[0:128:16, :], T.th[:]), [], ["thi"])
    op(S, "g", lambda: g.affine_select(T.blk1[:], T.ones[:], [[-16, 8], [0, 16]], A.is_ge, 0.0, 0, 1), ["ones"], ["blk1"])
    op(S, "g", lambda: g.affine_select(T.blk[:], T.blk1[:], [[16, 8], [0, 16]], A.is_ge, 0.0, 15, -1), ["blk1"], ["blk"])
    op(S, "g", lambda: g.affine_select(T.eye[:], T.ones[:], [[-1, 128]], A.is_equal, 0.0, 0, 1), ["ones"], ["eye"])
    vs(T.p15i[:], T.pidx[:], 15, None, A.bitwise_and, None, ["pidx"], ["p15i"])
    vs(T.gpi[:], T.pidx[:], 4, 1, A.arith_shift_right, A.bitwise_and, ["pidx"], ["gpi"])
    v(lambda: V.tensor_copy(T.p15[:], T.p15i[:]), ["p15i"], ["p15"])
    v(lambda: V.tensor_copy(T.gp1[:], T.gpi[:]), ["gpi"], ["gp1"])
    vs(T.gp0[:], T.gpi[:], -1.0, 1.0, A.mult, A.add, ["gpi"], ["gp0"])
    for i in range(16):
        copy(T.wd[:, i, i::16], T.blk[:, 0::16], ["blk", "wd"], [("wd", i, i + 1)])
    v(lambda: V.tensor_copy(T.wf[:], T.wti[:]), ["wti"], ["wf"])
    for gs in range(2):
        for c0 in range(4):
            vs(T.lh[:, gs * 4 + c0, c0::32], T.blk[:, 16 * gs::32], T.wf[:, 0:1], 2.0, A.mult, A.mult,
               ["blk", "wf"], [("lh", 2 * (gs * 4 + c0), 2 * (gs * 4 + c0) + 1)])
    vs(T.lu[:, 0:16], T.lfi[:], T.gp0[:, 0:1], None, A.mult, None, ["lfi", "gp0"], [("lu", 0, 16)])
    vs(T.lu[:, 16:32], T.lfi[:], T.gp1[:, 0:1], None, A.mult, None, ["lfi", "gp1"], [("lu", 16, 32)])
    v(lambda: V.transpose(T.lt[:], T.lu[:]), ["lu"], ["lt"])
    vt(T.fi[:], T.lt[:, 0:16], T.lt[:, 16:32], A.add, ["lt"], ["fi"])
    send(nxt, T.wp[:], T.wf[:], "wp", ["wf"])
    arrival(S, "wp", E, ["wp"])

    def rest_one():
        vs(T.neye[:], T.eye[:], -1.0, None, A.mult, None, ["eye"], ["neye"])
        vs(T.eye2[:], T.eye[:], 2.0, None, A.mult, None, ["eye"], ["eye2"])
        mm(T.pd[:, 0:16, 0], T.blk[:], T.zz[:], True, True, ["blk", "zz"], ["pd"])
        op(S, "g", lambda: g.iota(T.e16[:], [[16, 16]], 3840, 0, allow_small_or_imprecise_dtypes=True), [], ["e16"])
        op(S, "g", lambda: g.iota(T.hc[:], [[16384, 16], [0, 16]], 16400, 0, allow_small_or_imprecise_dtypes=True), [], ["hc"])
        for k in range(1, 16):
            op(S, "g", lambda: g.affine_select(T.sh[:, k - 1, :, k:16], T.neye[:, :, k:16], [[-16, 8], [-1, 16 - k]], A.not_equal,
                                               1.0, 0, 1), ["neye"], [("sh", 2 * k, 2 * k + 1)])

    def rest_two():
        vs(T.e3[:, 15::16], T.e16[:], T.p15[:, 0:1], None, A.add, None, ["e16", "p15"], ["e3"])
        v(lambda: V.tensor_copy(T.thb[:], T.thi[:]), ["thi"], ["thb"])
        mm(T.px[:, 0:1], T.blk[:], T.thb[:], True, True, ["blk", "thb"], ["px"])
        v(lambda: V.tensor_copy(T.thc[:], T.px[:, 0:1]), ["px"], ["thc"])

    def lhb():
        for gs in range(2):
            for c0 in range(4):
                q = gs * 4 + c0
                copy(T.lh[:, q, 16 + c0::32], T.blk[:, 16 * gs::32], ["blk", "wp"], [("lh", 2 * q + 1, 2 * q + 2)], scale=T.wp[:, 1:2])

    def chain(t):
        zi, ad = "zi%d" % t, "add%d" % t

        def sums():
            copy(T.z2[:], T[zi][:], [zi], ["z2"])
            for gs in range(2):
                for c0 in range(4):
                    q = gs * 4 + c0
                    mm(T.pg[:, :, gs, :], T.lh[:, q, :], T[zi][:, :, c0, :], c0 == 0, c0 == 3,
                       [("lh", 2 * q, 2 * q + (2 if t else 1)), zi], ["pg"])
            v(lambda: V.transpose(T.ts[:], T.pg[:, :, 0:2, :]), ["pg"], ["ts"])

        def rdoub():
            vs(T.rr[:, 0:16], T.qi[:], 296.0, None, A.add, None, ["qi"], [("rr", 0, 16)])
            for n in (16, 32, 64, 128):
                copy(T.rr[:, n:2 * n], T.rr[:, 0:n], [("rr", 0, n)], [("rr", n, 2 * n)])

        def sdoub(k, n):
            return lambda: vs(T.ss[:, n:2 * n], T.ss[:, 0:n], k, None, A.arith_shift_right, None, [("ss", 0, n)], [("ss", n, 2 * n)])

        def fwd():
            fw, to = "fw%d" % t, "add%d" % (t + 1)
            vs(T[fw][:, :, 1, :], T.fi[:], 8.0, None, A.mult, None, ["fi"], [fw])
            send(nxt, T[to][:], T[fw][:], "fa%d" % (t + 1), [fw])
            arrival(S, "fa%d" % (t + 1), E, [to])

        s0 = ("ss", 0, 64)
        out = [sums, lambda: vt(T.oi[:], T.ts[:, :, :, 0, :], T[ad][:], A.add, ["ts", ad], ["oi"])]
        if t:
            out.append(lambda: vs(T.fi[:], T.oi[:, :, 1, :], 32767, None, A.bitwise_and, None, ["oi"], ["fi"]))
        out += [lambda: vs(T.qi[:], T.oi[:, :, 0, :], 511, None, A.bitwise_and, None, ["oi"], ["qi"]),
                lambda: vs(T.ss[:, 0:16], T.fi[:], 32768.0, None, A.add, None, ["fi"], [("ss", 0, 16)]),
                rdoub, sdoub(1, 16), sdoub(2, 32), sdoub(4, 64), sdoub(8, 128)]
        if t < 4:
            out.append(fwd)
        out += [lambda: vs(T.bi[:], T.ss[:, 0:64], 4096, None, A.bitwise_and, None, [s0], ["bi"]),
                lambda: vs(T.ss[:, 0:64], T.ss[:, 0:64], 4095, None, A.bitwise_and, None, [s0], [s0]),
                lambda: vs(T.b8[:], T.bi[:], 8.0, None, A.mult, None, ["bi"], ["b8"]),
                lambda: vs(T.sp[:], T.ss[:], 2452.0, None, A.add, None, ["ss"], ["sp"]),
                lambda: vt(T.aa[:], T.sp[:], T.rr[:], A.mult, ["sp", "rr"], ["aa"]),
                lambda: vt(T.aa[:, 0:64], T.aa[:, 0:64], T.b8[:], A.add, ["aa", "b8"], [("aa", 0, 64)]),
                lambda: vs(T.ww[:], T.aa[:], 0.125, -91030.9375, A.mult, A.add, ["aa"], ["ww"]),
                lambda: vs(T.hh[:], T.ww[:], 8191, None, A.bitwise_and, None, ["ww"], ["hh"]),
                lambda: vs(T.li[:], T.hh[:], 16.0, None, A.add, None, ["hh"], ["li"])]
        return out

    def gather(t):
        ends = {5: (10, 16), 10: (5, 10), 14: (1, 5)}
        for k in [15] + list(range(15)):
            kk = 15 - k
            d = ("diff", 256 * kk, 256 * kk + 256)
            vt(T.diff[:, 256 * kk:256 * kk + 256], T.win[:, 0:CB].indirect(T.li[:, 16 * k:16 * k + 16]), T.z2[:], A.subtract,
               [("win", 0, CB), "li", "z2"], [d])
            if k < 15:
                s(lambda: C.activation(T.ad[:, :, kk], T.diff[:, 256 * kk:256 * kk + 256], F.Abs), [d], [("ad", kk, kk + 1)])
                if t == 0:
                    copy(T.sh[:, k, :, 0:k + 1], T.neye[:, :, 0:k + 1], ["neye"], [("sh", 2 * k + 3, 2 * k + 4)])
            if k == 7 and t == 0:
                rest_two()
            if k in ends:
                a, b = ends[k]
                for i in range(16):
                    mm(T.pd[:, 0:16, a:b], T.wd[:, i, :], T.ad[:, i::16, a:b], i == 0, i == 15,
                       [("wd", i, i + 1), ("ad", a, b)], ["pd"])
            if k == 1:
                vt(T.hf[:], T.hh[:], T.hc[:], A.add, ["hh", "hc"], ["hf"])
                vs(T.nr[:, 16:32], T.hh[:, 240:256], 16.0, None, A.add, None, ["hh"], [("nr", 16, 32)])
                for m in range(15):
                    op(S, "g", lambda: g.affine_select(T.hd[:, 15 - m::16], T.hf[:, 16 * m:16 * m + 16], [[0, 16]], A.is_gt, 0.0, 1, 0),
                       ["hf"], [("hd", 15 - m, 16 - m)])
            if k == 6:
                mm(T.pr[:, 0:256], T.eye[:], T.diff[:, 0:256], True, False, ["eye", ("diff", 0, 256)], ["pr"])
                mm(T.pr[:, 0:256], T.eye2[:], T.z2[:], False, True, ["eye2", "z2"], ["pr"])

    def answer(t):
        zn, mc = "zn%d" % t, "mc" if t else "thc"
        vs(T.ms[:], T.pd[:, 0:16, :], T[mc][:, 0:1], None, A.is_gt, None, ["pd", mc], ["ms"])
        v(lambda: V.tensor_tensor_scan(T.sc[:], T.ms[:], T.e3[:], 0.0, A.mult, A.add), ["ms", "e3"], ["sc"])
        v(lambda: V.tensor_copy(T.lo[:], T.sc[:, 15::16]), ["sc"], ["lo"])
        s(lambda: C.activation(T[zn][:], T.diff[:, 0:4096].indirect(T.lo[:]), F.Abs), ["diff", "lo"], [zn])
        if t < 4:
            send(nxt, T["zi%d" % (t + 1)][:], T[zn][:], "za%d" % (t + 1), [zn])
            arrival(S, "za%d" % (t + 1), E, ["zi%d" % (t + 1)])
        if t in (1, 2):
            send(cores[(rank - t) % N], T["zh%d" % t][:], T[zn][:], "h%d" % t, [zn])
        if t in (0, 4):
            dma(S, "y", lambda: g.sync.dma_start(T.zs[:, 256 * t:256 * t + 256], T[zn][:]), [zn], [])

    def update(t):
        n16 = ("nr", 0, 16)
        v(lambda: V.tensor_tensor_scan(T.sn[:], T.hd[:], T.ms[:], 0.0, A.max, A.mult), ["hd", "ms"], ["sn"])
        v(lambda: V.tensor_copy(T.ri[:], T.sn[:, 15::16]), ["sn"], ["ri"])
        vt(T.yv[:], T.diff[:, 0:4096].indirect(T.lo[:]), T.z2[:], A.add, ["diff", "lo", "z2"], ["yv"])
        vs(T.rn[:], T.ri[:], 16383, None, A.bitwise_and, None, ["ri"], ["rn"])
        if t < 4:
            vs(T.j15[:], T.sc[:, 15::16], 255.5, None, A.is_lt, None, ["sc"], ["j15"])
        vs(T.nr[:, 0:16], T.rn[:], T.p15[:, 0:1], None, A.max, None, ["rn", "p15"], [n16])
        v(lambda: V.tensor_copy(T.hl[:, 0:32], T.nr[:]), ["nr"], [("hl", 0, 32)])
        v(lambda: V.tensor_copy(T.nl[:], T.nr[:, 0:16]), [n16], ["nl"])
        vt(T.hl[:, 32:64], T.nr[:], T.hl[:, 0:32], A.subtract, ["nr", ("hl", 0, 32)], [("hl", 32, 64)])
        copy(T.nc[:], T.win[:, CB:NW].indirect(T.nl[:]), [("win", CB, NW), "nl"], ["nc"], bias=1.0, scale=-1.0)
        copy(T.vals[:, :, 0:16], T.yv[:], ["yv"], [("vals", 0, 1)])
        copy(T.vals[:, :, 16:32], T.nc[:], ["nc"], [("vals", 1, 2)])
        copy(T.rw[:], T.pr[:, 0:256], ["pr"], ["rw"], bias=127.8, scale=0.5)
        copy(T.rv[:], T.rw[:], ["rw"], ["rv"], bias=-128.0)
        if t == 0:
            lhb()
        if t == 1:
            copy(T.xa[:], T.wd[:], ["wd", "wf"], ["xa"], scale=T.wf[:, 0:1])
        for k in range(15):
            for h in range(2):
                mm(T.pq[:, k, :], T.sh[:, k, :, :], T.hl[:, 32 * h:32 * h + 32], h == 0, h == 1,
                   [("sh", 2 * k + 2, 2 * k + 4), ("hl", 32 * h, 32 * h + 32)], ["pq"])
        if t < 4:
            mm(T.px[:, 0:16], T.ones[:], T.j15[:], True, True, ["ones", "j15"], ["px"])
        vs(T.eq[:], T.pq[:, 0:15, :], 0.0, None, A.is_equal, None, ["pq"], ["eq"])
        for i in range(16):
            mm(T.pn[:, 0:16], T.wd[:, i, :], T.nc[:, i::16], i == 0, i == 15, ["wd", "nc"], ["pn"])
        for k in range(15):
            mm(T.pf[:, 0:32], T.eye[:], T.eq[:, k, :], k == 0, k == 14, ["eye", "eq"], ["pf"])
        if t < 4:
            v(lambda: V.tensor_reduce(T.ac[:], T.px[:, 0:16], AxisListType.X, A.add), ["px"], ["ac"])
            v(lambda: V.tensor_copy(T.ai[:], T.ac[:]), ["ac"], ["ai"])
            vs(T.am[:], T.ai[:], 15, None, A.bitwise_and, None, ["ai"], ["am"])
            vs(T.mc[:], T.am[:], T.thc[:, 0:1], None, A.add, None, ["am", "thc"], ["mc"])
        vs(T.u2[:], T.pn[:, 0:16], 0.5, None, A.is_lt, None, ["pn"], ["u2"])
        vs(T.uu[:], T.pf[:, 0:32], 0.5, None, A.is_lt, None, ["pf"], ["uu"])
        vt(T.un[:], T.uu[:], T.nr[:], A.mult, ["uu", "nr"], ["un"])
        vt(T.ur[:], T.un[:, 0:16], T.u2[:], A.mult, ["un", "u2"], ["ur"])
        vs(T.rl[:, 1::2], T.un[:, 0:16], T.p15[:, 0:1], float(CB), A.max, A.add, ["un", "p15"], [("rl", 1, 2)])
        vs(T.rt[:, 0::2], T.un[:, 16:32], T.p15[:, 0:1], None, A.max, None, ["un", "p15"], ["rt"])
        vs(T.rl[:, 0::2], T.ur[:], T.p15[:, 0:1], None, A.max, None, ["ur", "p15"], [("rl", 0, 1)])
        return [lambda c=c: v(lambda: V.tensor_copy(T.win[:, 0:NW].indirect(T.rl[:, 2 * c:2 * c + 2]), T.vals[:, c, :]),
                              ["rl", "vals"], ["win"]) for c in range(15, -1, -1)] + \
               [lambda c=c: v(lambda: V.tensor_copy(T.win[:, 0:CB].indirect(T.rt[:, 2 * c:2 * c + 1]), T.rv[:, 16 * c:16 * c + 16]),
                              ["rt", "rv"], [("win", 0, CB)]) for c in range(15, -1, -1)]

    for f in chain(0):
        f()
    rest_one()
    for t in range(5):
        gather(t)
        answer(t)
        sc = update(t)
        ch = chain(t + 1) if t < 4 else []
        for _ in range(6):
            sc.pop(0)()
        while ch or sc:
            if ch:
                ch.pop(0)()
            for _ in range(2 if len(sc) > len(ch) else 1):
                if sc:
                    sc.pop(0)()
    for q in range(16):
        mm(T.px[:], T.xa[:, q, :], T.win[:, 16 + 512 * q:528 + 512 * q], q == 0, q == 15, ["xa", ("win", 0, CB)], ["px"])
    v(lambda: V.tensor_copy(T.xo[:], T.px[:]), ["px"], ["xo"])
    dma(S, "g", lambda: g.dma_start(T.cs[:], T.win[0:128:16, CB + 16:NW]), [("win", CB, NW)], [], "gd")
    for t, b, sem in ((1, "zh1", "h1"), (2, "zh2", "h2")):
        arrival(S, sem, len(topo.engines(cores[(rank + t) % N], core)), [b])
        dma(S, "y", lambda: g.sync.dma_start(T.zs[:, 256 * t:256 * t + 256], T[b][:]), [b], [])
    dma(S, "y", lambda: g.sync.dma_start(T.zs[:, 768:1024], T.zi4[:]), ["zi4"], [])
    dma(S, "y", lambda: g.sync.dma_start(T.xs[:], T.xo[:]), ["xo"], [])
    for sem in SEMAPHORES:
        if S["count"].get(sem, 0):
            need(S, "g", (sem, S["count"][sem], {}))
